import numpy as np
import ml_dtypes


def mxq(x, axis, fmt="e4m3"):
    dtype, down = {"e4m3": (ml_dtypes.float8_e4m3fn, 7), "e5m2": (ml_dtypes.float8_e5m2, 14)}[fmt]
    v = np.moveaxis(np.asarray(x, np.float32).astype(ml_dtypes.bfloat16).astype(np.float64), axis, -1)
    blocks = v.reshape(v.shape[:-1] + (-1, 32))
    amax = np.abs(blocks).max(-1, keepdims=True)
    byte = np.maximum(np.where(amax > 0, np.frexp(amax)[1] - 1 + 127, 0) - down, 1)
    scale = np.exp2(byte - 127.0)
    codes = (blocks / scale).astype(np.float32).astype(dtype).astype(np.float64)
    return np.moveaxis((codes * scale).reshape(v.shape), -1, axis)


WIDE = False


def mx_kscale(k):
    if not WIDE:
        return np.ones(k)
    levels = np.array([10, -10, 5, -5, 0])
    if k % 512:
        return np.exp2(np.random.permutation(np.resize(levels, k // 32))).repeat(32)
    a = np.empty((k // 512, 16))
    for p in range(k // 512):
        a[p, :8] = np.random.permutation(np.resize(levels, 8))
        for g in range(8):
            far = levels[np.abs(levels - a[p, g]) >= 10]
            a[p, g + 8] = far[np.random.randint(len(far))]
    return np.exp2(a.ravel()).repeat(32)


def f64(x):
    return np.asarray(x).astype(np.float64)


def striped(idx):
    return np.tile(idx.reshape(-1, 16).T, (8, 1)).astype(np.uint16)


def unstriped(offs):
    return offs[:16].T.reshape(-1).astype(np.int64)


E2M1 = np.array([0.0, 0.5, 1.0, 1.5, 2.0, 3.0, 4.0, 6.0, -0.0, -0.5, -1.0, -1.5, -2.0, -3.0, -4.0, -6.0])


def pack_weight(w, fmt):
    k, n = w.shape
    w = f64(np.asarray(w, np.float32).astype(ml_dtypes.bfloat16)).reshape(k // 32, 32, n)
    amax = np.abs(w).max(1)
    if fmt == "e4m3":
        byte = np.frexp(amax)[1] - 1 + 127 - 7
    else:
        mant, ex = np.frexp(amax / 6.0)
        byte = np.where(mant > 0.5, ex, ex - 1) + 127
    byte = np.clip(np.where(amax > 0, byte, 1), 1, 254)
    scaled = (w * np.exp2(127.0 - byte)[:, None, :]).reshape(k, n).astype(np.float32)
    by_word = np.ascontiguousarray(scaled.reshape(k // 512, 128, 4, n).transpose(0, 1, 3, 2))
    if fmt == "e4m3":
        words = by_word.astype(ml_dtypes.float8_e4m3fn).view(np.uint8)
    else:
        c = by_word.astype(ml_dtypes.float4_e2m1fn).view(np.uint8) & 0xF
        words = (c[..., 0::2] | (c[..., 1::2] << 4)).reshape(k // 512, 128, 2 * n)
    return np.ascontiguousarray(words), np.ascontiguousarray(byte.astype(np.uint8).reshape(k // 512, 16, n))


def unpack_weight(words, scales, fmt):
    g, _, n = scales.shape
    words = np.ascontiguousarray(words).reshape(g, 128, n, -1)
    if fmt == "e4m3":
        vals = words.view(ml_dtypes.float8_e4m3fn).astype(np.float64)
    else:
        nib = np.empty((g, 128, n, 4), np.uint8)
        nib[..., 0::2] = words & 0xF
        nib[..., 1::2] = words >> 4
        vals = E2M1[nib]
    vals = vals * np.repeat(np.exp2(scales.astype(np.float64) - 127.0), 8, axis=1)[..., None]
    return vals.transpose(0, 1, 3, 2).reshape(g * 512, n)


def gelu(v):
    return 0.5 * v * (1.0 + np.tanh(np.sqrt(2.0 / np.pi) * (v + 0.044715 * v**3)))


K, T, S, H, S2, T3, T2 = 512, 4096, 1024, 1024, 512, 2048, 2048

def setup_inputs():
    n = np.random.standard_normal
    s = mx_kscale(K)[:, None]
    u = mx_kscale(H)[:, None]
    tab_words, tab_scales = pack_weight(n((K, T)) * s, "e4m3")
    w2_words, w2_scales = pack_weight(n((K, H)) / np.sqrt(K) / s * u.T, "e2m1")
    tab2_words, tab2_scales = pack_weight(n((H, T3)) / np.sqrt(H) / u, "e4m3")
    return {
        "tab_words": tab_words, "tab_scales": tab_scales,
        "offs": striped(np.random.permutation(T)[:S]),
        "w1": (n((K, H)) / np.sqrt(K) / s * u.T).astype(np.float32),
        "w2_words": w2_words, "w2_scales": w2_scales,
        "w3": (n((K, H)) / np.sqrt(K) / s * u.T).astype(np.float32),
        "tab2_words": tab2_words, "tab2_scales": tab2_scales,
        "offs2": striped(np.random.permutation(T3)[:S2]),
        "cond": np.exp(0.4 * n((S2, S))).astype(np.float32),
        "athlete": (0.7 * n(S2)).astype(np.float32),
        "page1": n((S2, T2)).astype(np.float32),
        "wgo": np.exp(0.3 * n((128, S))).astype(np.float32),
        "offs3": striped(np.random.permutation(T2)[:S]),
    }

def reference(tab_words, tab_scales, offs, w1, w2_words, w2_scales, w3, tab2_words, tab2_scales, offs2, cond, athlete, page1, wgo, offs3):
    v = unpack_weight(tab_words, tab_scales, "e4m3")[:, unstriped(offs)]
    v2 = unpack_weight(tab2_words, tab2_scales, "e4m3")[:, unstriped(offs2)]
    a1 = mxq(f64(w1), 0, "e4m3").T @ v
    a2 = unpack_weight(w2_words, w2_scales, "e2m1").T @ v
    a3 = mxq(f64(w3), 0, "e4m3").T @ v
    h = np.maximum(a1, a2) + np.minimum(a2, a3)
    e = v2.T @ mxq(h, 0, "e4m3")
    y = np.tanh(f64(cond) * e + f64(athlete)[:, None])
    out = f64(page1).copy()
    out[:, unstriped(offs3)] = np.tile(f64(wgo), (S2 // 128, 1)) * y
    return out

@@ -1,0 +1,240 @@
+from contextlib import ExitStack
+
+import concourse.mybir as mybir
+from concourse.masks import make_identity
+
+K, T, S, H, S2, T3, T2 = 512, 4096, 1024, 1024, 512, 2048, 2048
+FLOPS = 2 * (3 * K * H * S + H * S2 * S)
+
+F32 = mybir.dt.float32
+BF16 = mybir.dt.bfloat16
+I32 = mybir.dt.int32
+U32 = mybir.dt.uint32
+U16 = mybir.dt.uint16
+U8 = mybir.dt.uint8
+FP8X4 = mybir.dt.float8_e4m3fn_x4
+FP4X4 = mybir.dt.float4_e2m1fn_x4
+ALU = mybir.AluOpType
+ACT = mybir.ActivationFunctionType
+
+P = 128
+PACK = 4
+RQ = 256
+JH = 512
+N_RQ = H // RQ
+N_JH = S // JH
+N_MT = S2 // P
+N_PASS = H // (P * PACK)
+
+
+def tile_list_pentathlon_points_revision_kernel(
+    tc, tab_words, tab_scales, offs, w1, w2_words, w2_scales, w3, tab2_words, tab2_scales,
+    offs2, cond, athlete, page1, wgo, offs3, out,
+):
+    nc = tc.nc
+    with ExitStack() as ctx:
+        lists = ctx.enter_context(tc.tile_pool(name="lists", bufs=1))
+        keep = ctx.enter_context(tc.tile_pool(name="keep", bufs=1))
+        ring = ctx.enter_context(tc.tile_pool(name="ring", bufs=2))
+        psum = ctx.enter_context(tc.psum_pool(name="psum", bufs=1))
+
+        idx = lists.tile([P, S // 16], U16, name="idx")
+        idx2 = lists.tile([P, S2 // 16], U16, name="idx2")
+        idx3 = lists.tile([P, S // 16], U16, name="idx3")
+
+        tab_w = keep.tile([P, T], I32, name="tab_w", align_bytes=64)
+        tab_s = keep.tile([P, T], U8, name="tab_s", align_bytes=64)
+        tab2_w = [keep.tile([P, T3], I32, name="tab2_w%d" % a, align_bytes=64) for a in range(N_PASS)]
+        tab2_s = keep.tile([P, T3], U8, name="tab2_s", align_bytes=64)
+        w2_w = keep.tile([P, 2 * H], U8, name="w2_w", align_bytes=64)
+        w2_s = keep.tile([P, H], U8, name="w2_s", align_bytes=64)
+        ident = keep.tile([P, P], F32, name="ident")
+        ath = keep.tile([P, N_MT], F32, name="ath")
+        wgo_t = keep.tile([P, S], F32, name="wgo_t")
+        cond_t = [keep.tile([P, S], F32, name="cond%d" % m) for m in range(N_MT)]
+        page = [keep.tile([P, T2], F32, name="page%d" % m) for m in range(N_MT)]
+
+        nc.vector.memset(tab_s[:].bitcast(I32), 0)
+        nc.vector.memset(w2_s[:].bitcast(I32), 0)
+        nc.vector.memset(tab2_s[:].bitcast(I32), 0)
+        make_identity(nc, ident[:])
+
+        w_raw = {}
+
+        def load_w(q):
+            for n, w in enumerate((w1, w3)):
+                raw = ring.tile([P, PACK, RQ], F32, name="w_raw", bufs=8)
+                nc.sync.dma_start(out=raw[:], in_=w.rearrange("(p i) c -> p i c", i=PACK)[:, :, q * RQ:(q + 1) * RQ])
+                w_raw[n, q] = raw
+
+        nc.sync.dma_start(idx[:], offs)
+        nc.sync.dma_start(out=tab_w[:], in_=tab_words[0].rearrange("p t i -> p (t i)").bitcast(I32))
+        for g in range(4):
+            nc.sync.dma_start(out=tab_s[32 * g:32 * g + 4, :].bitcast(I32), in_=tab_scales[0, 4 * g:4 * g + 4, :].bitcast(I32))
+        load_w(0)
+        nc.sync.dma_start(out=w2_w[:].bitcast(I32), in_=w2_words[0].bitcast(I32))
+        for g in range(4):
+            nc.sync.dma_start(out=w2_s[32 * g:32 * g + 4, :].bitcast(I32), in_=w2_scales[0, 4 * g:4 * g + 4, :].bitcast(I32))
+        for q in range(1, N_RQ):
+            load_w(q)
+
+        def load_rows(m):
+            nc.sync.dma_start(out=cond_t[m][:], in_=cond[m * P:(m + 1) * P, :])
+            nc.sync.dma_start(out=page[m][:], in_=page1[m * P:(m + 1) * P, :])
+
+        nc.sync.dma_start(idx2[:], offs2)
+        nc.sync.dma_start(idx3[:], offs3)
+        with nc.allow_non_contiguous_dma(reason="one value of athlete for each partition"):
+            nc.sync.dma_start(out=ath[:], in_=athlete.rearrange("(m p) -> p m", p=P))
+        nc.sync.dma_start(out=wgo_t[:], in_=wgo)
+        load_rows(0)
+        load_rows(1)
+        for a in range(N_PASS):
+            nc.sync.dma_start(out=tab2_w[a][:], in_=tab2_words[a].rearrange("p t i -> p (t i)").bitcast(I32))
+        for g in range(4):
+            nc.sync.dma_start(out=tab2_s[32 * g:32 * g + 8, :].bitcast(I32), in_=tab2_scales[:, 4 * g:4 * g + 4, :].bitcast(I32))
+        load_rows(2)
+        load_rows(3)
+
+        v_w, v_s = {}, {}
+
+        def gather_v(jh):
+            o = idx[:, jh * JH // 16:(jh + 1) * JH // 16]
+            v_w[jh] = keep.tile([P, JH], U32, name="v_w%d" % jh, align_bytes=64)
+            v_s[jh] = keep.tile([P, JH], U8, name="v_s%d" % jh, align_bytes=64)
+            nc.vector.tensor_copy(v_w[jh][:], tab_w[:].bitcast(U32).indirect(o))
+            nc.vector.tensor_copy(v_s[jh][:], tab_s[:].indirect(o))
+
+        v2_w = [keep.tile([P, S2], U32, name="v2_w%d" % a, align_bytes=64) for a in range(N_PASS)]
+        v2_s = keep.tile([P, S2], U8, name="v2_s", align_bytes=64)
+
+        def gather_v2():
+            for a in range(N_PASS):
+                nc.vector.tensor_copy(v2_w[a][:], tab2_w[a][:].bitcast(U32).indirect(idx2[:]))
+            nc.vector.tensor_copy(v2_s[:], tab2_s[:].indirect(idx2[:]))
+
+        w_c, w_s = {}, {}
+
+        def quantize_w(q):
+            for n in range(2):
+                wb = ring.tile([P, RQ, PACK], BF16, name="w_bf", bufs=3, align_bytes=64)
+                nc.scalar.copy(
+                    out=wb[:].rearrange("p (c k) i -> p c i k", k=4),
+                    in_=w_raw[n, q][:].rearrange("p i (c k) -> p c i k", k=4),
+                )
+                w_c[n, q] = keep.tile([P, RQ], U32, name="w_c%d_%d" % (n, q), align_bytes=64)
+                w_s[n, q] = keep.tile([P, RQ], U8, name="w_s%d_%d" % (n, q), align_bytes=64)
+                nc.vector.quantize_mx(out=w_c[n, q][:].bitcast(FP8X4), scales=w_s[n, q][:], in_=wb[:].rearrange("p c i -> p (c i)"))
+
+        hi, lo = {}, {}
+
+        def stage1(jp, q):
+            jh, rh, half = jp // 2, q // 2, q % 2
+            if half == 0:
+                hi[jp, rh] = ring.tile([P, 2, PACK, P], F32, name="hi", bufs=6)
+                lo[jp, rh] = ring.tile([P, 2, PACK, P], F32, name="lo", bufs=6)
+            a1 = psum.tile([P, 2, RQ], F32, name="a1", bufs=2)
+            a2 = psum.tile([P, 2, RQ], F32, name="a2", bufs=1)
+            a3 = psum.tile([P, 2, RQ], F32, name="a3", bufs=2)
+            moving = (
+                (a2, w2_w[:, 2 * q * RQ:2 * (q + 1) * RQ].bitcast(FP4X4), w2_s[:, q * RQ:(q + 1) * RQ]),
+                (a1, w_c[0, q][:].bitcast(FP8X4), w_s[0, q][:]),
+                (a3, w_c[1, q][:].bitcast(FP8X4), w_s[1, q][:]),
+            )
+            for bank, codes, scales in moving:
+                for b in range(2):
+                    cols = slice((jp % 2) * 2 * P + b * P, (jp % 2) * 2 * P + (b + 1) * P)
+                    nc.tensor.matmul_mx(
+                        out=bank[:, b, :], lhsT=v_w[jh][:, cols].bitcast(FP8X4), lhsT_scale=v_s[jh][:, cols],
+                        rhs=codes, rhs_scale=scales, start=True, stop=True,
+                    )
+            a2_sb = ring.tile([P, 2, PACK, RQ // PACK], F32, name="a2_sb", bufs=3)
+            nc.scalar.copy(out=a2_sb[:], in_=a2[:].rearrange("p b (m t) -> p b t m", t=PACK))
+            ms = slice(half * (RQ // PACK), (half + 1) * (RQ // PACK))
+            nc.vector.tensor_tensor(hi[jp, rh][:, :, :, ms], a1[:].rearrange("p b (m t) -> p b t m", t=PACK), a2_sb[:], ALU.max)
+            nc.vector.tensor_tensor(lo[jp, rh][:, :, :, ms], a3[:].rearrange("p b (m t) -> p b t m", t=PACK), a2_sb[:], ALU.min)
+
+        h_bf = {}
+
+        def turn(jp, rh):
+            h_bf[jp, rh] = ring.tile([P, 2 * P, PACK], BF16, name="h_bf", bufs=4, align_bytes=64)
+            for b in range(2):
+                ht = psum.tile([P, PACK, P], F32, name="ht", bufs=2)
+                for t in range(PACK):
+                    nc.tensor.matmul(ht[:, t, :], hi[jp, rh][:, b, t, :], ident[:], start=True, stop=False, is_transpose=True)
+                    nc.tensor.matmul(ht[:, t, :], lo[jp, rh][:, b, t, :], ident[:], start=False, stop=True, is_transpose=True)
+                nc.scalar.copy(out=h_bf[jp, rh][:, b * P:(b + 1) * P, :], in_=ht[:].rearrange("p t n -> p n t"))
+
+        h_c, h_s = {}, {}
+
+        def quantize_h(jp, rh):
+            jh = jp // 2
+            if jp % 2 == 0:
+                h_c[jh, rh] = keep.tile([P, JH], U32, name="h_c%d_%d" % (jh, rh), align_bytes=64)
+                h_s[jh, rh] = keep.tile([P, JH], U8, name="h_s%d_%d" % (jh, rh), align_bytes=64)
+            cols = slice((jp % 2) * 2 * P, (jp % 2 + 1) * 2 * P)
+            nc.vector.quantize_mx(out=h_c[jh, rh][:, cols].bitcast(FP8X4), scales=h_s[jh, rh][:, cols], in_=h_bf[jp, rh][:].rearrange("p j t -> p (j t)"))
+
+        ys = {}
+
+        def score(jh, m):
+            e = psum.tile([P, JH], F32, name="e", bufs=1)
+            cols = slice(m * P, (m + 1) * P)
+            for a in range(N_PASS):
+                nc.tensor.matmul_mx(
+                    out=e[:], lhsT=v2_w[a][:, cols].bitcast(FP8X4), lhsT_scale=v2_s[4 * a:P, cols],
+                    rhs=h_c[jh, a][:].bitcast(FP8X4), rhs_scale=h_s[jh, a][:], start=(a == 0), stop=(a == N_PASS - 1),
+                )
+            js = slice(jh * JH, (jh + 1) * JH)
+            z = ring.tile([P, JH], F32, name="z", bufs=2)
+            nc.vector.tensor_tensor(z[:], e[:], cond_t[m][:, js], ALU.mult)
+            y = ring.tile([P, JH], F32, name="y", bufs=3)
+            nc.scalar.activation(out=y[:], in_=z[:], func=ACT.Tanh, bias=ath[:, m:m + 1])
+            ys[jh, m] = y
+
+        def put(jh, m):
+            js = slice(jh * JH, (jh + 1) * JH)
+            o = idx3[:, jh * JH // 16:(jh + 1) * JH // 16]
+            nc.vector.tensor_tensor(page[m][:].indirect(o), ys[jh, m][:], wgo_t[:, js], ALU.mult)
+            if jh == N_JH - 1:
+                nc.sync.dma_start(out=out[m * P:(m + 1) * P, :], in_=page[m][:])
+
+        gather_v(0)
+        quantize_w(0)
+        gather_v(1)
+        for q in range(N_RQ - 1):
+            for jp in range(4):
+                if jp == 3:
+                    quantize_w(q + 1)
+                stage1(jp, q)
+                if q == 1 and jp in (1, 3):
+                    turn(jp // 2, 0)
+                if q == 2 and jp in (0, 1):
+                    quantize_h(jp, 0)
+        stage1(0, 3)
+        stage1(1, 3)
+        turn(0, 1)
+        turn(1, 1)
+        gather_v2()
+        quantize_h(0, 1)
+        quantize_h(1, 1)
+        stage1(2, 3)
+        score(0, 0)
+        stage1(3, 3)
+        score(0, 1)
+        late = [(2, 0), (3, 0), (2, 1), (3, 1)]
+        steps = [(jh, m) for jh in range(N_JH) for m in range(N_MT)]
+        turn(*late[0])
+        turn(*late[1])
+        for n, (jh, m) in enumerate(steps):
+            put(jh, m)
+            if n == 0:
+                quantize_h(*late[0])
+                quantize_h(*late[1])
+                turn(*late[2])
+                turn(*late[3])
+            if n == 1:
+                quantize_h(*late[2])
+                quantize_h(*late[3])
+            if n + 2 < len(steps):
+                score(*steps[n + 2])

@@ -19,12 +19,24 @@ ACT = mybir.ActivationFunctionType
 
 P = 128
 PACK = 4
-RQ = 256
-JH = 512
-N_RQ = H // RQ
-N_JH = S // JH
-N_MT = S2 // P
+QUADS = 4
+LIST_ROWS = 16
+CHUNK = 256
+PAIR = 2 * P
+HALF = 512
+N_CHUNK = H // CHUNK
+N_PAIR = S // PAIR
+N_HALF = S // HALF
+N_ROWS = S2 // P
 N_PASS = H // (P * PACK)
+CHUNK_M = CHUNK // PACK
+
+BANKS = 2
+MINMAX_BUFS = 6
+A2_BUFS = 4
+CAST_BUFS = 3
+H_BUFS = 4
+Z_BUFS = 3
 
 
 def tile_list_pentathlon_points_revision_kernel(
@@ -38,78 +50,89 @@ def tile_list_pentathlon_points_revision_kernel(
         ring = ctx.enter_context(tc.tile_pool(name="ring", bufs=2))
         psum = ctx.enter_context(tc.psum_pool(name="psum", bufs=1))
 
-        idx = lists.tile([P, S // 16], U16, name="idx")
-        idx2 = lists.tile([P, S2 // 16], U16, name="idx2")
-        idx3 = lists.tile([P, S // 16], U16, name="idx3")
+        idx = lists.tile([P, S // LIST_ROWS], U16, name="idx")
+        idx2 = lists.tile([P, S2 // LIST_ROWS], U16, name="idx2")
+        idx3 = lists.tile([P, S // LIST_ROWS], U16, name="idx3")
 
         tab_w = keep.tile([P, T], I32, name="tab_w", align_bytes=64)
         tab_s = keep.tile([P, T], U8, name="tab_s", align_bytes=64)
         tab2_w = [keep.tile([P, T3], I32, name="tab2_w%d" % a, align_bytes=64) for a in range(N_PASS)]
         tab2_s = keep.tile([P, T3], U8, name="tab2_s", align_bytes=64)
-        w2_w = keep.tile([P, 2 * H], U8, name="w2_w", align_bytes=64)
         w2_s = keep.tile([P, H], U8, name="w2_s", align_bytes=64)
         ident = keep.tile([P, P], F32, name="ident")
-        ath = keep.tile([P, N_MT], F32, name="ath")
+        ath = keep.tile([P, N_ROWS], F32, name="ath")
         wgo_t = keep.tile([P, S], F32, name="wgo_t")
-        cond_t = [keep.tile([P, S], F32, name="cond%d" % m) for m in range(N_MT)]
-        page = [keep.tile([P, T2], F32, name="page%d" % m) for m in range(N_MT)]
+        cond_t = [keep.tile([P, S], F32, name="cond%d" % m) for m in range(N_ROWS)]
+        page = [keep.tile([P, T2], F32, name="page%d" % m) for m in range(N_ROWS)]
+
+        def load_scale_rows(queue, tile, scales):
+            rows = 4 * scales.shape[0]
+            for g in range(QUADS):
+                queue.dma_start(
+                    out=tile[32 * g:32 * g + rows, :].bitcast(I32), in_=scales[:, 4 * g:4 * g + 4, :].bitcast(I32)
+                )
 
         nc.vector.memset(tab_s[:].bitcast(I32), 0)
-        nc.vector.memset(w2_s[:].bitcast(I32), 0)
         nc.vector.memset(tab2_s[:].bitcast(I32), 0)
+        nc.gpsimd.memset(w2_s[:].bitcast(I32), 0)
+        load_scale_rows(nc.gpsimd, w2_s, w2_scales)
         make_identity(nc, ident[:])
+        ath_rows = keep.tile([P, P], F32, name="ath_rows")
+        nc.gpsimd.memset(ath_rows[:], 0.0)
 
         w_raw = {}
 
-        def load_w(q):
+        def load_w(first, end):
             for n, w in enumerate((w1, w3)):
-                raw = ring.tile([P, PACK, RQ], F32, name="w_raw", bufs=8)
-                nc.sync.dma_start(out=raw[:], in_=w.rearrange("(p i) c -> p i c", i=PACK)[:, :, q * RQ:(q + 1) * RQ])
-                w_raw[n, q] = raw
+                raw = keep.tile([P, PACK, (end - first) * CHUNK], F32, name="w_raw%d_%d" % (n, first))
+                nc.sync.dma_start(
+                    out=raw[:], in_=w.rearrange("(p i) c -> p i c", i=PACK)[:, :, first * CHUNK:end * CHUNK]
+                )
+                for q in range(first, end):
+                    w_raw[n, q] = raw[:, :, (q - first) * CHUNK:(q - first + 1) * CHUNK]
 
         nc.sync.dma_start(idx[:], offs)
         nc.sync.dma_start(out=tab_w[:], in_=tab_words[0].rearrange("p t i -> p (t i)").bitcast(I32))
-        for g in range(4):
-            nc.sync.dma_start(out=tab_s[32 * g:32 * g + 4, :].bitcast(I32), in_=tab_scales[0, 4 * g:4 * g + 4, :].bitcast(I32))
-        load_w(0)
+        load_scale_rows(nc.sync, tab_s, tab_scales)
+        load_w(0, 1)
+        w2_w = keep.tile([P, 2 * H], U8, name="w2_w", align_bytes=64)
         nc.sync.dma_start(out=w2_w[:].bitcast(I32), in_=w2_words[0].bitcast(I32))
-        for g in range(4):
-            nc.sync.dma_start(out=w2_s[32 * g:32 * g + 4, :].bitcast(I32), in_=w2_scales[0, 4 * g:4 * g + 4, :].bitcast(I32))
-        for q in range(1, N_RQ):
-            load_w(q)
-
-        def load_rows(m):
+        load_w(1, 2)
+        load_w(2, N_CHUNK)
+        nc.sync.dma_start(idx2[:], offs2)
+        nc.sync.dma_start(idx3[:], offs3)
+        nc.sync.dma_start(out=ath_rows[0:N_ROWS, :], in_=athlete.rearrange("(m p) -> m p", p=P))
+        load_scale_rows(nc.sync, tab2_s, tab2_scales)
+        for a in range(N_PASS):
+            nc.sync.dma_start(out=tab2_w[a][:], in_=tab2_words[a].rearrange("p t i -> p (t i)").bitcast(I32))
+        nc.sync.dma_start(out=wgo_t[:], in_=wgo)
+        for m in range(N_ROWS):
             nc.sync.dma_start(out=cond_t[m][:], in_=cond[m * P:(m + 1) * P, :])
             nc.sync.dma_start(out=page[m][:], in_=page1[m * P:(m + 1) * P, :])
 
-        nc.sync.dma_start(idx2[:], offs2)
-        nc.sync.dma_start(idx3[:], offs3)
-        with nc.allow_non_contiguous_dma(reason="one value of athlete for each partition"):
-            nc.sync.dma_start(out=ath[:], in_=athlete.rearrange("(m p) -> p m", p=P))
-        nc.sync.dma_start(out=wgo_t[:], in_=wgo)
-        load_rows(0)
-        load_rows(1)
-        for a in range(N_PASS):
-            nc.sync.dma_start(out=tab2_w[a][:], in_=tab2_words[a].rearrange("p t i -> p (t i)").bitcast(I32))
-        for g in range(4):
-            nc.sync.dma_start(out=tab2_s[32 * g:32 * g + 8, :].bitcast(I32), in_=tab2_scales[:, 4 * g:4 * g + 4, :].bitcast(I32))
-        load_rows(2)
-        load_rows(3)
+        def entries(tile, half):
+            return tile[:, half * HALF // LIST_ROWS:(half + 1) * HALF // LIST_ROWS]
+
+        def turn_athlete():
+            turned = psum.tile([P, P], F32, name="ath_turned", tag="turned", bufs=BANKS)
+            nc.tensor.transpose(turned[:], ath_rows[:], ident[:])
+            nc.scalar.copy(out=ath[:], in_=turned[:, 0:N_ROWS])
 
         v_w, v_s = {}, {}
 
-        def gather_v(jh):
-            o = idx[:, jh * JH // 16:(jh + 1) * JH // 16]
-            v_w[jh] = keep.tile([P, JH], U32, name="v_w%d" % jh, align_bytes=64)
-            v_s[jh] = keep.tile([P, JH], U8, name="v_s%d" % jh, align_bytes=64)
-            nc.vector.tensor_copy(v_w[jh][:], tab_w[:].bitcast(U32).indirect(o))
-            nc.vector.tensor_copy(v_s[jh][:], tab_s[:].indirect(o))
+        def gather_v(half):
+            v_w[half] = keep.tile([P, HALF], U32, name="v_w%d" % half, align_bytes=64)
+            tag = "v_s0" if half == 0 else "w_first"
+            v_s[half] = keep.tile([P, HALF], U8, name="v_s%d" % half, tag=tag, align_bytes=64)
+            nc.vector.tensor_copy(v_w[half][:], tab_w[:].bitcast(U32).indirect(entries(idx, half)))
+            nc.vector.tensor_copy(v_s[half][:], tab_s[:].indirect(entries(idx, half)))
 
-        v2_w = [keep.tile([P, S2], U32, name="v2_w%d" % a, align_bytes=64) for a in range(N_PASS)]
+        v2_w = {}
         v2_s = keep.tile([P, S2], U8, name="v2_s", align_bytes=64)
 
         def gather_v2():
             for a in range(N_PASS):
+                v2_w[a] = keep.tile([P, S2], U32, name="v2_w%d" % a, tag="a2_last%d" % a, align_bytes=64)
                 nc.vector.tensor_copy(v2_w[a][:], tab2_w[a][:].bitcast(U32).indirect(idx2[:]))
             nc.vector.tensor_copy(v2_s[:], tab2_s[:].indirect(idx2[:]))
 
@@ -117,124 +140,152 @@ def tile_list_pentathlon_points_revision_kernel(
 
         def quantize_w(q):
             for n in range(2):
-                wb = ring.tile([P, RQ, PACK], BF16, name="w_bf", bufs=3, align_bytes=64)
+                if (n, q) == (0, 0):
+                    w_bf = keep.tile([P, CHUNK, PACK], BF16, name="w_first", tag="w_first", align_bytes=64)
+                else:
+                    w_bf = ring.tile([P, CHUNK, PACK], BF16, name="w_bf", tag="w_bf", bufs=CAST_BUFS, align_bytes=64)
                 nc.scalar.copy(
-                    out=wb[:].rearrange("p (c k) i -> p c i k", k=4),
-                    in_=w_raw[n, q][:].rearrange("p i (c k) -> p c i k", k=4),
+                    out=w_bf[:].rearrange("p (c u) i -> p c i u", u=4),
+                    in_=w_raw[n, q].rearrange("p i (c u) -> p c i u", u=4),
                 )
-                w_c[n, q] = keep.tile([P, RQ], U32, name="w_c%d_%d" % (n, q), align_bytes=64)
-                w_s[n, q] = keep.tile([P, RQ], U8, name="w_s%d_%d" % (n, q), align_bytes=64)
-                nc.vector.quantize_mx(out=w_c[n, q][:].bitcast(FP8X4), scales=w_s[n, q][:], in_=wb[:].rearrange("p c i -> p (c i)"))
+                w_c[n, q] = keep.tile([P, CHUNK], U32, name="w_c%d_%d" % (n, q), align_bytes=64)
+                w_s[n, q] = keep.tile([P, CHUNK], U8, name="w_s%d_%d" % (n, q), align_bytes=64)
+                nc.vector.quantize_mx(
+                    out=w_c[n, q][:].bitcast(FP8X4), scales=w_s[n, q][:], in_=w_bf[:].rearrange("p c i -> p (c i)")
+                )
 
-        hi, lo = {}, {}
+        upper, lower = {}, {}
 
-        def stage1(jp, q):
-            jh, rh, half = jp // 2, q // 2, q % 2
-            if half == 0:
-                hi[jp, rh] = ring.tile([P, 2, PACK, P], F32, name="hi", bufs=6)
-                lo[jp, rh] = ring.tile([P, 2, PACK, P], F32, name="lo", bufs=6)
-            a1 = psum.tile([P, 2, RQ], F32, name="a1", bufs=2)
-            a2 = psum.tile([P, 2, RQ], F32, name="a2", bufs=1)
-            a3 = psum.tile([P, 2, RQ], F32, name="a3", bufs=2)
+        def stage1(pair, q, a1_tag="a1"):
+            half, a = pair // 2, q // 2
+            if q % 2 == 0:
+                upper[pair, a] = ring.tile([P, 2, PACK, P], F32, name="upper", bufs=MINMAX_BUFS)
+                lower[pair, a] = ring.tile([P, 2, PACK, P], F32, name="lower", bufs=MINMAX_BUFS)
+            a1 = psum.tile([P, 2, CHUNK], F32, name="a1", tag=a1_tag, bufs=BANKS)
+            a2 = psum.tile([P, 2, CHUNK], F32, name="a2", bufs=BANKS)
+            a3 = psum.tile([P, 2, CHUNK], F32, name="a3", tag="a3", bufs=BANKS)
             moving = (
-                (a2, w2_w[:, 2 * q * RQ:2 * (q + 1) * RQ].bitcast(FP4X4), w2_s[:, q * RQ:(q + 1) * RQ]),
+                (a2, w2_w[:, 2 * q * CHUNK:2 * (q + 1) * CHUNK].bitcast(FP4X4), w2_s[:, q * CHUNK:(q + 1) * CHUNK]),
                 (a1, w_c[0, q][:].bitcast(FP8X4), w_s[0, q][:]),
                 (a3, w_c[1, q][:].bitcast(FP8X4), w_s[1, q][:]),
             )
             for bank, codes, scales in moving:
                 for b in range(2):
-                    cols = slice((jp % 2) * 2 * P + b * P, (jp % 2) * 2 * P + (b + 1) * P)
+                    cols = slice((pair % 2) * PAIR + b * P, (pair % 2) * PAIR + (b + 1) * P)
                     nc.tensor.matmul_mx(
-                        out=bank[:, b, :], lhsT=v_w[jh][:, cols].bitcast(FP8X4), lhsT_scale=v_s[jh][:, cols],
+                        out=bank[:, b, :], lhsT=v_w[half][:, cols].bitcast(FP8X4), lhsT_scale=v_s[half][:, cols],
                         rhs=codes, rhs_scale=scales, start=True, stop=True,
                     )
-            a2_sb = ring.tile([P, 2, PACK, RQ // PACK], F32, name="a2_sb", bufs=3)
+            if q == N_CHUNK - 1 and half == 0:
+                a2_sb = keep.tile([P, 2, PACK, CHUNK_M], F32, name="a2_last", tag="a2_last%d" % pair, align_bytes=64)
+            else:
+                a2_sb = ring.tile([P, 2, PACK, CHUNK_M], F32, name="a2_sb", tag="a2_sb", bufs=A2_BUFS)
             nc.scalar.copy(out=a2_sb[:], in_=a2[:].rearrange("p b (m t) -> p b t m", t=PACK))
-            ms = slice(half * (RQ // PACK), (half + 1) * (RQ // PACK))
-            nc.vector.tensor_tensor(hi[jp, rh][:, :, :, ms], a1[:].rearrange("p b (m t) -> p b t m", t=PACK), a2_sb[:], ALU.max)
-            nc.vector.tensor_tensor(lo[jp, rh][:, :, :, ms], a3[:].rearrange("p b (m t) -> p b t m", t=PACK), a2_sb[:], ALU.min)
+            ms = slice((q % 2) * CHUNK_M, (q % 2 + 1) * CHUNK_M)
+            nc.vector.tensor_tensor(
+                upper[pair, a][:, :, :, ms], a1[:].rearrange("p b (m t) -> p b t m", t=PACK), a2_sb[:], ALU.max
+            )
+            nc.vector.tensor_tensor(
+                lower[pair, a][:, :, :, ms], a3[:].rearrange("p b (m t) -> p b t m", t=PACK), a2_sb[:], ALU.min
+            )
 
         h_bf = {}
 
-        def turn(jp, rh):
-            h_bf[jp, rh] = ring.tile([P, 2 * P, PACK], BF16, name="h_bf", bufs=4, align_bytes=64)
+        def turn(pair, a):
+            h_bf[pair, a] = ring.tile([P, PAIR, PACK], BF16, name="h_bf", bufs=H_BUFS, align_bytes=64)
             for b in range(2):
-                ht = psum.tile([P, PACK, P], F32, name="ht", bufs=2)
+                turned = psum.tile([P, PACK, P], F32, name="h_turned", tag="turned", bufs=BANKS)
                 for t in range(PACK):
-                    nc.tensor.matmul(ht[:, t, :], hi[jp, rh][:, b, t, :], ident[:], start=True, stop=False, is_transpose=True)
-                    nc.tensor.matmul(ht[:, t, :], lo[jp, rh][:, b, t, :], ident[:], start=False, stop=True, is_transpose=True)
-                nc.scalar.copy(out=h_bf[jp, rh][:, b * P:(b + 1) * P, :], in_=ht[:].rearrange("p t n -> p n t"))
+                    nc.tensor.matmul(
+                        turned[:, t, :], upper[pair, a][:, b, t, :], ident[:], start=True, stop=False, is_transpose=True
+                    )
+                    nc.tensor.matmul(
+                        turned[:, t, :], lower[pair, a][:, b, t, :], ident[:], start=False, stop=True, is_transpose=True
+                    )
+                nc.scalar.copy(out=h_bf[pair, a][:, b * P:(b + 1) * P, :], in_=turned[:].rearrange("p t n -> p n t"))
 
         h_c, h_s = {}, {}
 
-        def quantize_h(jp, rh):
-            jh = jp // 2
-            if jp % 2 == 0:
-                h_c[jh, rh] = keep.tile([P, JH], U32, name="h_c%d_%d" % (jh, rh), align_bytes=64)
-                h_s[jh, rh] = keep.tile([P, JH], U8, name="h_s%d_%d" % (jh, rh), align_bytes=64)
-            cols = slice((jp % 2) * 2 * P, (jp % 2 + 1) * 2 * P)
-            nc.vector.quantize_mx(out=h_c[jh, rh][:, cols].bitcast(FP8X4), scales=h_s[jh, rh][:, cols], in_=h_bf[jp, rh][:].rearrange("p j t -> p (j t)"))
+        def quantize_h(pair, a):
+            half = pair // 2
+            if pair % 2 == 0:
+                h_c[half, a] = keep.tile([P, HALF], U32, name="h_c%d_%d" % (half, a), align_bytes=64)
+                h_s[half, a] = keep.tile([P, HALF], U8, name="h_s%d_%d" % (half, a), align_bytes=64)
+            cols = slice((pair % 2) * PAIR, (pair % 2 + 1) * PAIR)
+            nc.vector.quantize_mx(
+                out=h_c[half, a][:, cols].bitcast(FP8X4), scales=h_s[half, a][:, cols],
+                in_=h_bf[pair, a][:].rearrange("p j t -> p (j t)"),
+            )
 
         ys = {}
 
-        def score(jh, m):
-            e = psum.tile([P, JH], F32, name="e", bufs=1)
+        def score(half, m):
+            e = psum.tile([P, HALF], F32, name="e", tag=("a1", "a3")[m % 2], bufs=BANKS)
             cols = slice(m * P, (m + 1) * P)
             for a in range(N_PASS):
                 nc.tensor.matmul_mx(
                     out=e[:], lhsT=v2_w[a][:, cols].bitcast(FP8X4), lhsT_scale=v2_s[4 * a:P, cols],
-                    rhs=h_c[jh, a][:].bitcast(FP8X4), rhs_scale=h_s[jh, a][:], start=(a == 0), stop=(a == N_PASS - 1),
+                    rhs=h_c[half, a][:].bitcast(FP8X4), rhs_scale=h_s[half, a][:],
+                    start=(a == 0), stop=(a == N_PASS - 1),
                 )
-            js = slice(jh * JH, (jh + 1) * JH)
-            z = ring.tile([P, JH], F32, name="z", bufs=2)
-            nc.vector.tensor_tensor(z[:], e[:], cond_t[m][:, js], ALU.mult)
-            y = ring.tile([P, JH], F32, name="y", bufs=3)
+            z = ring.tile([P, HALF], F32, name="z", bufs=Z_BUFS)
+            nc.vector.tensor_tensor(z[:], e[:], cond_t[m][:, half * HALF:(half + 1) * HALF], ALU.mult)
+            y = ring.tile([P, HALF], F32, name="y", tag="w_bf", bufs=CAST_BUFS, align_bytes=64)
             nc.scalar.activation(out=y[:], in_=z[:], func=ACT.Tanh, bias=ath[:, m:m + 1])
-            ys[jh, m] = y
+            ys[half, m] = y
 
-        def put(jh, m):
-            js = slice(jh * JH, (jh + 1) * JH)
-            o = idx3[:, jh * JH // 16:(jh + 1) * JH // 16]
-            nc.vector.tensor_tensor(page[m][:].indirect(o), ys[jh, m][:], wgo_t[:, js], ALU.mult)
-            if jh == N_JH - 1:
+        def put(half, m):
+            nc.vector.tensor_tensor(
+                page[m][:].indirect(entries(idx3, half)), ys[half, m][:],
+                wgo_t[:, half * HALF:(half + 1) * HALF], ALU.mult,
+            )
+            if half == N_HALF - 1:
                 nc.sync.dma_start(out=out[m * P:(m + 1) * P, :], in_=page[m][:])
+
+        first_pairs, second_pairs = (0, 1), (2, 3)
 
         gather_v(0)
         quantize_w(0)
         gather_v(1)
-        for q in range(N_RQ - 1):
-            for jp in range(4):
-                if jp == 3:
+        for q in range(2):
+            for pair in range(N_PAIR):
+                if pair == N_PAIR - 1:
                     quantize_w(q + 1)
-                stage1(jp, q)
-                if q == 1 and jp in (1, 3):
-                    turn(jp // 2, 0)
-                if q == 2 and jp in (0, 1):
-                    quantize_h(jp, 0)
-        stage1(0, 3)
-        stage1(1, 3)
-        turn(0, 1)
-        turn(1, 1)
+                stage1(pair, q)
+
+        stage1(0, 2)
+        quantize_w(3)
+        stage1(1, 2)
+        for pair in first_pairs:
+            turn(pair, 0)
+        for pair in first_pairs:
+            stage1(pair, 3)
+        for pair in first_pairs:
+            quantize_h(pair, 0)
+        turn_athlete()
         gather_v2()
-        quantize_h(0, 1)
-        quantize_h(1, 1)
+        for pair in first_pairs:
+            turn(pair, 1)
+
+        for pair in second_pairs:
+            stage1(pair, 2)
         stage1(2, 3)
-        score(0, 0)
-        stage1(3, 3)
-        score(0, 1)
-        late = [(2, 0), (3, 0), (2, 1), (3, 1)]
-        steps = [(jh, m) for jh in range(N_JH) for m in range(N_MT)]
-        turn(*late[0])
-        turn(*late[1])
-        for n, (jh, m) in enumerate(steps):
-            put(jh, m)
-            if n == 0:
-                quantize_h(*late[0])
-                quantize_h(*late[1])
-                turn(*late[2])
-                turn(*late[3])
-            if n == 1:
-                quantize_h(*late[2])
-                quantize_h(*late[3])
-            if n + 2 < len(steps):
+        for pair in first_pairs:
+            quantize_h(pair, 1)
+        stage1(3, 3, a1_tag="turned")
+        for pair in second_pairs:
+            turn(pair, 0)
+        for pair in second_pairs:
+            quantize_h(pair, 0)
+        for pair in second_pairs:
+            turn(pair, 1)
+        for m in range(N_ROWS):
+            score(0, m)
+        for pair in second_pairs:
+            quantize_h(pair, 1)
+
+        steps = [(half, m) for half in range(N_HALF) for m in range(N_ROWS)]
+        for n, step in enumerate(steps):
+            if N_ROWS <= n + 2 < len(steps):
                 score(*steps[n + 2])
+            put(*step)

from contextlib import ExitStack

import concourse.mybir as mybir
from concourse.masks import make_identity

K, T, S, H, S2, T3, T2 = 512, 4096, 1024, 1024, 512, 2048, 2048
FLOPS = 2 * (3 * K * H * S + H * S2 * S)

F32 = mybir.dt.float32
BF16 = mybir.dt.bfloat16
I32 = mybir.dt.int32
U32 = mybir.dt.uint32
U16 = mybir.dt.uint16
U8 = mybir.dt.uint8
FP8X4 = mybir.dt.float8_e4m3fn_x4
FP4X4 = mybir.dt.float4_e2m1fn_x4
ALU = mybir.AluOpType
ACT = mybir.ActivationFunctionType

P = 128
PACK = 4
QUADS = 4
LIST_ROWS = 16
CHUNK = 256
PAIR = 2 * P
HALF = 512
N_CHUNK = H // CHUNK
N_PAIR = S // PAIR
N_HALF = S // HALF
N_ROWS = S2 // P
N_PASS = H // (P * PACK)
CHUNK_M = CHUNK // PACK

BANKS = 2
MINMAX_BUFS = 6
A2_BUFS = 4
CAST_BUFS = 3
H_BUFS = 4
Z_BUFS = 3


def tile_list_pentathlon_points_revision_kernel(
    tc, tab_words, tab_scales, offs, w1, w2_words, w2_scales, w3, tab2_words, tab2_scales,
    offs2, cond, athlete, page1, wgo, offs3, out,
):
    nc = tc.nc
    with ExitStack() as ctx:
        lists = ctx.enter_context(tc.tile_pool(name="lists", bufs=1))
        keep = ctx.enter_context(tc.tile_pool(name="keep", bufs=1))
        ring = ctx.enter_context(tc.tile_pool(name="ring", bufs=2))
        psum = ctx.enter_context(tc.psum_pool(name="psum", bufs=1))

        idx = lists.tile([P, S // LIST_ROWS], U16, name="idx")
        idx2 = lists.tile([P, S2 // LIST_ROWS], U16, name="idx2")
        idx3 = lists.tile([P, S // LIST_ROWS], U16, name="idx3")

        tab_w = keep.tile([P, T], I32, name="tab_w", align_bytes=64)
        tab_s = keep.tile([P, T], U8, name="tab_s", align_bytes=64)
        tab2_w = [keep.tile([P, T3], I32, name="tab2_w%d" % a, align_bytes=64) for a in range(N_PASS)]
        tab2_s = keep.tile([P, T3], U8, name="tab2_s", align_bytes=64)
        w2_s = keep.tile([P, H], U8, name="w2_s", align_bytes=64)
        ident = keep.tile([P, P], F32, name="ident")
        ath = keep.tile([P, N_ROWS], F32, name="ath")
        wgo_t = keep.tile([P, S], F32, name="wgo_t")
        cond_t = [keep.tile([P, S], F32, name="cond%d" % m) for m in range(N_ROWS)]
        page = [keep.tile([P, T2], F32, name="page%d" % m) for m in range(N_ROWS)]

        def load_scale_rows(queue, tile, scales):
            rows = 4 * scales.shape[0]
            for g in range(QUADS):
                queue.dma_start(
                    out=tile[32 * g:32 * g + rows, :].bitcast(I32), in_=scales[:, 4 * g:4 * g + 4, :].bitcast(I32)
                )

        nc.vector.memset(tab_s[:].bitcast(I32), 0)
        nc.vector.memset(tab2_s[:].bitcast(I32), 0)
        nc.gpsimd.memset(w2_s[:].bitcast(I32), 0)
        load_scale_rows(nc.gpsimd, w2_s, w2_scales)
        make_identity(nc, ident[:])
        ath_rows = keep.tile([P, P], F32, name="ath_rows")
        nc.gpsimd.memset(ath_rows[:], 0.0)

        w_raw = {}

        def load_w(first, end):
            for n, w in enumerate((w1, w3)):
                raw = keep.tile([P, PACK, (end - first) * CHUNK], F32, name="w_raw%d_%d" % (n, first))
                nc.sync.dma_start(
                    out=raw[:], in_=w.rearrange("(p i) c -> p i c", i=PACK)[:, :, first * CHUNK:end * CHUNK]
                )
                for q in range(first, end):
                    w_raw[n, q] = raw[:, :, (q - first) * CHUNK:(q - first + 1) * CHUNK]

        nc.sync.dma_start(idx[:], offs)
        nc.sync.dma_start(out=tab_w[:], in_=tab_words[0].rearrange("p t i -> p (t i)").bitcast(I32))
        load_scale_rows(nc.sync, tab_s, tab_scales)
        load_w(0, 1)
        w2_w = keep.tile([P, 2 * H], U8, name="w2_w", align_bytes=64)
        nc.sync.dma_start(out=w2_w[:].bitcast(I32), in_=w2_words[0].bitcast(I32))
        load_w(1, 2)
        load_w(2, N_CHUNK)
        nc.sync.dma_start(idx2[:], offs2)
        nc.sync.dma_start(idx3[:], offs3)
        nc.sync.dma_start(out=ath_rows[0:N_ROWS, :], in_=athlete.rearrange("(m p) -> m p", p=P))
        load_scale_rows(nc.sync, tab2_s, tab2_scales)
        for a in range(N_PASS):
            nc.sync.dma_start(out=tab2_w[a][:], in_=tab2_words[a].rearrange("p t i -> p (t i)").bitcast(I32))
        nc.sync.dma_start(out=wgo_t[:], in_=wgo)
        for m in range(N_ROWS):
            nc.sync.dma_start(out=cond_t[m][:], in_=cond[m * P:(m + 1) * P, :])
            nc.sync.dma_start(out=page[m][:], in_=page1[m * P:(m + 1) * P, :])

        def entries(tile, half):
            return tile[:, half * HALF // LIST_ROWS:(half + 1) * HALF // LIST_ROWS]

        def turn_athlete():
            turned = psum.tile([P, P], F32, name="ath_turned", tag="turned", bufs=BANKS)
            nc.tensor.transpose(turned[:], ath_rows[:], ident[:])
            nc.scalar.copy(out=ath[:], in_=turned[:, 0:N_ROWS])

        v_w, v_s = {}, {}

        def gather_v(half):
            v_w[half] = keep.tile([P, HALF], U32, name="v_w%d" % half, align_bytes=64)
            tag = "v_s0" if half == 0 else "w_first"
            v_s[half] = keep.tile([P, HALF], U8, name="v_s%d" % half, tag=tag, align_bytes=64)
            nc.vector.tensor_copy(v_w[half][:], tab_w[:].bitcast(U32).indirect(entries(idx, half)))
            nc.vector.tensor_copy(v_s[half][:], tab_s[:].indirect(entries(idx, half)))

        v2_w = {}
        v2_s = keep.tile([P, S2], U8, name="v2_s", align_bytes=64)

        def gather_v2():
            for a in range(N_PASS):
                v2_w[a] = keep.tile([P, S2], U32, name="v2_w%d" % a, tag="a2_last%d" % a, align_bytes=64)
                nc.vector.tensor_copy(v2_w[a][:], tab2_w[a][:].bitcast(U32).indirect(idx2[:]))
            nc.vector.tensor_copy(v2_s[:], tab2_s[:].indirect(idx2[:]))

        w_c, w_s = {}, {}

        def quantize_w(q):
            for n in range(2):
                if (n, q) == (0, 0):
                    w_bf = keep.tile([P, CHUNK, PACK], BF16, name="w_first", tag="w_first", align_bytes=64)
                else:
                    w_bf = ring.tile([P, CHUNK, PACK], BF16, name="w_bf", tag="w_bf", bufs=CAST_BUFS, align_bytes=64)
                nc.scalar.copy(
                    out=w_bf[:].rearrange("p (c u) i -> p c i u", u=4),
                    in_=w_raw[n, q].rearrange("p i (c u) -> p c i u", u=4),
                )
                w_c[n, q] = keep.tile([P, CHUNK], U32, name="w_c%d_%d" % (n, q), align_bytes=64)
                w_s[n, q] = keep.tile([P, CHUNK], U8, name="w_s%d_%d" % (n, q), align_bytes=64)
                nc.vector.quantize_mx(
                    out=w_c[n, q][:].bitcast(FP8X4), scales=w_s[n, q][:], in_=w_bf[:].rearrange("p c i -> p (c i)")
                )

        upper, lower = {}, {}

        def stage1(pair, q, a1_tag="a1"):
            half, a = pair // 2, q // 2
            if q % 2 == 0:
                upper[pair, a] = ring.tile([P, 2, PACK, P], F32, name="upper", bufs=MINMAX_BUFS)
                lower[pair, a] = ring.tile([P, 2, PACK, P], F32, name="lower", bufs=MINMAX_BUFS)
            a1 = psum.tile([P, 2, CHUNK], F32, name="a1", tag=a1_tag, bufs=BANKS)
            a2 = psum.tile([P, 2, CHUNK], F32, name="a2", bufs=BANKS)
            a3 = psum.tile([P, 2, CHUNK], F32, name="a3", tag="a3", bufs=BANKS)
            moving = (
                (a2, w2_w[:, 2 * q * CHUNK:2 * (q + 1) * CHUNK].bitcast(FP4X4), w2_s[:, q * CHUNK:(q + 1) * CHUNK]),
                (a1, w_c[0, q][:].bitcast(FP8X4), w_s[0, q][:]),
                (a3, w_c[1, q][:].bitcast(FP8X4), w_s[1, q][:]),
            )
            for bank, codes, scales in moving:
                for b in range(2):
                    cols = slice((pair % 2) * PAIR + b * P, (pair % 2) * PAIR + (b + 1) * P)
                    nc.tensor.matmul_mx(
                        out=bank[:, b, :], lhsT=v_w[half][:, cols].bitcast(FP8X4), lhsT_scale=v_s[half][:, cols],
                        rhs=codes, rhs_scale=scales, start=True, stop=True,
                    )
            if q == N_CHUNK - 1 and half == 0:
                a2_sb = keep.tile([P, 2, PACK, CHUNK_M], F32, name="a2_last", tag="a2_last%d" % pair, align_bytes=64)
            else:
                a2_sb = ring.tile([P, 2, PACK, CHUNK_M], F32, name="a2_sb", tag="a2_sb", bufs=A2_BUFS)
            nc.scalar.copy(out=a2_sb[:], in_=a2[:].rearrange("p b (m t) -> p b t m", t=PACK))
            ms = slice((q % 2) * CHUNK_M, (q % 2 + 1) * CHUNK_M)
            nc.vector.tensor_tensor(
                upper[pair, a][:, :, :, ms], a1[:].rearrange("p b (m t) -> p b t m", t=PACK), a2_sb[:], ALU.max
            )
            nc.vector.tensor_tensor(
                lower[pair, a][:, :, :, ms], a3[:].rearrange("p b (m t) -> p b t m", t=PACK), a2_sb[:], ALU.min
            )

        h_bf = {}

        def turn(pair, a):
            h_bf[pair, a] = ring.tile([P, PAIR, PACK], BF16, name="h_bf", bufs=H_BUFS, align_bytes=64)
            for b in range(2):
                turned = psum.tile([P, PACK, P], F32, name="h_turned", tag="turned", bufs=BANKS)
                for t in range(PACK):
                    nc.tensor.matmul(
                        turned[:, t, :], upper[pair, a][:, b, t, :], ident[:], start=True, stop=False, is_transpose=True
                    )
                    nc.tensor.matmul(
                        turned[:, t, :], lower[pair, a][:, b, t, :], ident[:], start=False, stop=True, is_transpose=True
                    )
                nc.scalar.copy(out=h_bf[pair, a][:, b * P:(b + 1) * P, :], in_=turned[:].rearrange("p t n -> p n t"))

        h_c, h_s = {}, {}

        def quantize_h(pair, a):
            half = pair // 2
            if pair % 2 == 0:
                h_c[half, a] = keep.tile([P, HALF], U32, name="h_c%d_%d" % (half, a), align_bytes=64)
                h_s[half, a] = keep.tile([P, HALF], U8, name="h_s%d_%d" % (half, a), align_bytes=64)
            cols = slice((pair % 2) * PAIR, (pair % 2 + 1) * PAIR)
            nc.vector.quantize_mx(
                out=h_c[half, a][:, cols].bitcast(FP8X4), scales=h_s[half, a][:, cols],
                in_=h_bf[pair, a][:].rearrange("p j t -> p (j t)"),
            )

        ys = {}

        def score(half, m):
            e = psum.tile([P, HALF], F32, name="e", tag=("a1", "a3")[m % 2], bufs=BANKS)
            cols = slice(m * P, (m + 1) * P)
            for a in range(N_PASS):
                nc.tensor.matmul_mx(
                    out=e[:], lhsT=v2_w[a][:, cols].bitcast(FP8X4), lhsT_scale=v2_s[4 * a:P, cols],
                    rhs=h_c[half, a][:].bitcast(FP8X4), rhs_scale=h_s[half, a][:],
                    start=(a == 0), stop=(a == N_PASS - 1),
                )
            z = ring.tile([P, HALF], F32, name="z", bufs=Z_BUFS)
            nc.vector.tensor_tensor(z[:], e[:], cond_t[m][:, half * HALF:(half + 1) * HALF], ALU.mult)
            y = ring.tile([P, HALF], F32, name="y", tag="w_bf", bufs=CAST_BUFS, align_bytes=64)
            nc.scalar.activation(out=y[:], in_=z[:], func=ACT.Tanh, bias=ath[:, m:m + 1])
            ys[half, m] = y

        def put(half, m):
            nc.vector.tensor_tensor(
                page[m][:].indirect(entries(idx3, half)), ys[half, m][:],
                wgo_t[:, half * HALF:(half + 1) * HALF], ALU.mult,
            )
            if half == N_HALF - 1:
                nc.sync.dma_start(out=out[m * P:(m + 1) * P, :], in_=page[m][:])

        first_pairs, second_pairs = (0, 1), (2, 3)

        gather_v(0)
        quantize_w(0)
        gather_v(1)
        for q in range(2):
            for pair in range(N_PAIR):
                if pair == N_PAIR - 1:
                    quantize_w(q + 1)
                stage1(pair, q)

        stage1(0, 2)
        quantize_w(3)
        stage1(1, 2)
        for pair in first_pairs:
            turn(pair, 0)
        for pair in first_pairs:
            stage1(pair, 3)
        for pair in first_pairs:
            quantize_h(pair, 0)
        turn_athlete()
        gather_v2()
        for pair in first_pairs:
            turn(pair, 1)

        for pair in second_pairs:
            stage1(pair, 2)
        stage1(2, 3)
        for pair in first_pairs:
            quantize_h(pair, 1)
        stage1(3, 3, a1_tag="turned")
        for pair in second_pairs:
            turn(pair, 0)
        for pair in second_pairs:
            quantize_h(pair, 0)
        for pair in second_pairs:
            turn(pair, 1)
        for m in range(N_ROWS):
            score(0, m)
        for pair in second_pairs:
            quantize_h(pair, 1)

        steps = [(half, m) for half in range(N_HALF) for m in range(N_ROWS)]
        for n, step in enumerate(steps):
            if N_ROWS <= n + 2 < len(steps):
                score(*steps[n + 2])
            put(*step)
